import numpy as np
import ml_dtypes


def mxq(x, axis, fmt="e4m3"):
    dtype, down = {"e4m3": (ml_dtypes.float8_e4m3fn, 7), "e5m2": (ml_dtypes.float8_e5m2, 14)}[fmt]
    v = np.moveaxis(np.asarray(x, np.float32).astype(ml_dtypes.bfloat16).astype(np.float64), axis, -1)
    blocks = v.reshape(v.shape[:-1] + (-1, 32))
    amax = np.abs(blocks).max(-1, keepdims=True)
    byte = np.maximum(np.where(amax > 0, np.frexp(amax)[1] - 1 + 127, 0) - down, 1)
    scale = np.exp2(byte - 127.0)
    codes = (blocks / scale).astype(np.float32).astype(dtype).astype(np.float64)
    return np.moveaxis((codes * scale).reshape(v.shape), -1, axis)


WIDE = False


def mx_kscale(k):
    if not WIDE:
        return np.ones(k)
    levels = np.array([10, -10, 5, -5, 0])
    if k % 512:
        return np.exp2(np.random.permutation(np.resize(levels, k // 32))).repeat(32)
    a = np.empty((k // 512, 16))
    for p in range(k // 512):
        a[p, :8] = np.random.permutation(np.resize(levels, 8))
        for g in range(8):
            far = levels[np.abs(levels - a[p, g]) >= 10]
            a[p, g + 8] = far[np.random.randint(len(far))]
    return np.exp2(a.ravel()).repeat(32)


def f64(x):
    return np.asarray(x).astype(np.float64)


def striped(idx):
    return np.tile(idx.reshape(-1, 16).T, (8, 1)).astype(np.uint16)


def unstriped(offs):
    return offs[:16].T.reshape(-1).astype(np.int64)


E2M1 = np.array([0.0, 0.5, 1.0, 1.5, 2.0, 3.0, 4.0, 6.0, -0.0, -0.5, -1.0, -1.5, -2.0, -3.0, -4.0, -6.0])


def pack_weight(w, fmt):
    k, n = w.shape
    w = f64(np.asarray(w, np.float32).astype(ml_dtypes.bfloat16)).reshape(k // 32, 32, n)
    amax = np.abs(w).max(1)
    if fmt == "e4m3":
        byte = np.frexp(amax)[1] - 1 + 127 - 7
    else:
        mant, ex = np.frexp(amax / 6.0)
        byte = np.where(mant > 0.5, ex, ex - 1) + 127
    byte = np.clip(np.where(amax > 0, byte, 1), 1, 254)
    scaled = (w * np.exp2(127.0 - byte)[:, None, :]).reshape(k, n).astype(np.float32)
    by_word = np.ascontiguousarray(scaled.reshape(k // 512, 128, 4, n).transpose(0, 1, 3, 2))
    if fmt == "e4m3":
        words = by_word.astype(ml_dtypes.float8_e4m3fn).view(np.uint8)
    else:
        c = by_word.astype(ml_dtypes.float4_e2m1fn).view(np.uint8) & 0xF
        words = (c[..., 0::2] | (c[..., 1::2] << 4)).reshape(k // 512, 128, 2 * n)
    return np.ascontiguousarray(words), np.ascontiguousarray(byte.astype(np.uint8).reshape(k // 512, 16, n))


def unpack_weight(words, scales, fmt):
    g, _, n = scales.shape
    words = np.ascontiguousarray(words).reshape(g, 128, n, -1)
    if fmt == "e4m3":
        vals = words.view(ml_dtypes.float8_e4m3fn).astype(np.float64)
    else:
        nib = np.empty((g, 128, n, 4), np.uint8)
        nib[..., 0::2] = words & 0xF
        nib[..., 1::2] = words >> 4
        vals = E2M1[nib]
    vals = vals * np.repeat(np.exp2(scales.astype(np.float64) - 127.0), 8, axis=1)[..., None]
    return vals.transpose(0, 1, 3, 2).reshape(g * 512, n)


def gelu(v):
    return 0.5 * v * (1.0 + np.tanh(np.sqrt(2.0 / np.pi) * (v + 0.044715 * v**3)))


K, T, E, C, N = 512, 1024, 16, 128, 384
TOP = 3
PAD = 64


def by_expert(wq, xq):
    return np.concatenate([wq[e].T @ xq[:, e * C:(e + 1) * C] for e in range(E)], axis=1)


def setup_inputs():
    n = np.random.standard_normal
    s = mx_kscale(K)[:, None]
    slot_token = np.empty(E * C, np.int64); pos = np.tile(E * C + np.arange(T) % PAD, (TOP, 1)); taken = np.zeros(T, np.int64)
    liked = np.random.randn(T)
    for e in np.random.permutation(E):
        free = np.flatnonzero(taken < TOP); pick = np.random.permutation(free[np.argsort(-(liked[free] + np.random.gumbel(size=free.size)))[:C]]); slot_token[e * C:(e + 1) * C] = pick
        pos[taken[pick], pick] = e * C + np.arange(C); taken[pick] += 1
    g = np.random.uniform(0.2, 0.8, (TOP, T))
    w = [pack_weight(m, "e2m1") for m in n((E, K, N)) / np.sqrt(K) / s[None]]
    return {
        "xT": (n((K, T)) * s).astype(np.float32),
        "w_words": np.stack([m[0] for m in w]),
        "w_scales": np.stack([m[1] for m in w]),
        "b": (0.3 * n((N, E))).astype(np.float32),
        "gate": np.stack([np.tile(r, (N, 1)) for r in g]).astype(np.float32),
        "offs": striped(slot_token),
        "pos1": striped(pos[0]),
        "pos2": striped(pos[1]),
        "pos3": striped(pos[2]),
    }


def reference(xT, w_words, w_scales, b, gate, offs, pos1, pos2, pos3):
    idx = unstriped(offs)
    w = np.stack([unpack_weight(w_words[e], w_scales[e], "e2m1") for e in range(E)])
    xq = mxq(f64(xT)[:, idx], 0, "e4m3")
    y = by_expert(w, xq)
    y = gelu(y + np.repeat(f64(b), C, axis=1))
    y = np.concatenate([y, np.zeros((N, PAD))], axis=1)
    return sum(f64(gate[r]) * y[:, unstriped(p)] for r, p in enumerate((pos1, pos2, pos3)))

@@ -1,0 +1,198 @@
+from contextlib import ExitStack
+
+import concourse.mybir as mybir
+from concourse.masks import make_identity
+
+K, T, E, C, N = 512, 1024, 16, 128, 384
+TOP = 3
+PAD = 64
+SLOTS = E * C
+FLOPS = 2 * K * N * SLOTS
+
+F32 = mybir.dt.float32
+BF16 = mybir.dt.bfloat16
+I32 = mybir.dt.int32
+U32 = mybir.dt.uint32
+U16 = mybir.dt.uint16
+U8 = mybir.dt.uint8
+FP8X4 = mybir.dt.float8_e4m3fn_x4
+FP4X4 = mybir.dt.float4_e2m1fn_x4
+GELU = mybir.ActivationFunctionType.Gelu_apprx_tanh
+MULT = mybir.AluOpType.mult
+ADD = mybir.AluOpType.add
+
+P = 128
+PACK = 4
+LIST_ROWS = 16
+BLOCKS = N // P
+BANK = 512
+
+X_LOADS = (512, 256, 256)
+GATHER_EXPERTS = (4, 4, 4, 3, 1)
+W_LOAD_EXPERTS = 8
+
+
+def tile_moe_ecr_lin_gelu_kernel(tc, xT, w_words, w_scales, b, gate, offs, pos1, pos2, pos3, out):
+    nc = tc.nc
+    with ExitStack() as ctx:
+        keep = ctx.enter_context(tc.tile_pool(name="keep", bufs=1))
+        work = ctx.enter_context(tc.tile_pool(name="work", bufs=3))
+        mm_psum = ctx.enter_context(tc.psum_pool(name="mm_psum", bufs=4))
+        sum_psum = ctx.enter_context(tc.psum_pool(name="sum_psum", bufs=2))
+        back_psum = ctx.enter_context(tc.psum_pool(name="back_psum", bufs=2))
+
+        w_scale = keep.tile([P, E, N], U8, align_bytes=64)
+        nc.vector.memset(w_scale[:].bitcast(I32), 0)
+        x_codes = keep.tile([P, T], U32, align_bytes=64)
+        x_scale = keep.tile([P, T], U8, align_bytes=64)
+        nc.vector.memset(x_scale[:].bitcast(I32), 0)
+        zeros = keep.tile([P, PAD], F32)
+        nc.vector.memset(zeros[:], 0.0)
+
+        x_rows = xT.rearrange("(p j) t -> p j t", j=PACK)
+        x_raw = []
+        t0 = 0
+        for i, width in enumerate(X_LOADS):
+            raw = keep.tile([P, PACK, width], F32, name="x_raw%d" % i)
+            nc.sync.dma_start(out=raw[:], in_=x_rows[:, :, t0 : t0 + width])
+            x_raw.append(raw)
+            t0 = t0 + width
+
+        slot_list = keep.tile([P, SLOTS // LIST_ROWS], U16)
+        nc.sync.dma_start(slot_list[:], offs)
+
+        for r in range(4):
+            nc.sync.dma_start(
+                out=w_scale[r:P:32, :, :].bitcast(I32),
+                in_=w_scales[:, 0, r:16:4, :].rearrange("e q n -> q e n").bitcast(I32),
+            )
+        w_code = []
+        for i in range(E // W_LOAD_EXPERTS):
+            wt = keep.tile([P, W_LOAD_EXPERTS, 2 * N], U8, name="w_code%d" % i, align_bytes=64)
+            nc.sync.dma_start(
+                out=wt[:].bitcast(I32),
+                in_=w_words[i * W_LOAD_EXPERTS : (i + 1) * W_LOAD_EXPERTS, 0, :, :].rearrange("e p c -> p e c").bitcast(I32),
+            )
+            w_code.append(wt)
+        bias = keep.tile([P, BLOCKS, E], F32)
+        nc.sync.dma_start(out=bias[:], in_=b.rearrange("(c p) e -> p c e", p=P))
+        pos_list = []
+        gate_rows = []
+        for r, pos in enumerate((pos1, pos2, pos3)):
+            pl = keep.tile([P, T // LIST_ROWS], U16, name="pos_list%d" % r)
+            nc.sync.dma_start(pl[:], pos)
+            pos_list.append(pl)
+            g = keep.tile([P, T], F32, name="gate_rows%d" % r)
+            nc.sync.dma_start(out=g[:], in_=gate[r, 0:P, :])
+            gate_rows.append(g)
+
+        ident = keep.tile([P, P], F32)
+        make_identity(nc, ident[:])
+
+        y = [keep.tile([P, SLOTS + PAD], F32, name="y%d" % nb) for nb in range(BLOCKS)]
+        for nb in range(BLOCKS):
+            nc.scalar.activation(y[nb][:, SLOTS:], zeros[:], GELU)
+
+        def interleave(copy, name, raw, c0, width):
+            grouped = keep.tile([P, width, PACK], BF16, name=name, align_bytes=64)
+            copy(
+                grouped[:].rearrange("p (c i) j -> p c j i", i=4),
+                raw[:, :, c0 : c0 + width].rearrange("p j (c i) -> p c j i", i=4),
+            )
+            return grouped
+
+        def quantize(grouped, t0, width):
+            nc.vector.quantize_mx(
+                out=x_codes[:, t0 : t0 + width].bitcast(FP8X4),
+                scales=x_scale[:, t0 : t0 + width],
+                in_=grouped[:].rearrange("p c j -> p (c j)"),
+            )
+
+        ga = interleave(nc.vector.tensor_copy, "ga", x_raw[0], 0, 512)
+        gb = interleave(nc.scalar.copy, "gb", x_raw[1], 0, 256)
+        quantize(ga, 0, 512)
+        gc = interleave(nc.vector.tensor_copy, "gc", x_raw[2], 0, 128)
+        gd = interleave(nc.scalar.copy, "gd", x_raw[2], 128, 128)
+        quantize(gb, 512, 256)
+        quantize(gc, 768, 128)
+        quantize(gd, 896, 128)
+
+        slot_codes = {}
+        slot_scale = {}
+
+        def expert_rows(experts, nb):
+            acc = mm_psum.tile([P, BANK], F32)
+            for i, e in enumerate(experts):
+                wt = w_code[e // W_LOAD_EXPERTS]
+                nc.tensor.matmul_mx(
+                    out=acc[:, i * C : (i + 1) * C],
+                    lhsT=wt[:, e % W_LOAD_EXPERTS, 2 * nb * P : 2 * (nb + 1) * P].bitcast(FP4X4),
+                    lhsT_scale=w_scale[:, e, nb * P : (nb + 1) * P],
+                    rhs=slot_codes[e].bitcast(FP8X4),
+                    rhs_scale=slot_scale[e],
+                    start=True,
+                    stop=True,
+                )
+            for i, e in enumerate(experts):
+                nc.scalar.activation(
+                    y[nb][:, e * C : (e + 1) * C], acc[:, i * C : (i + 1) * C], GELU, bias=bias[:, nb, e : e + 1]
+                )
+
+        e0 = 0
+        for i, count in enumerate(GATHER_EXPERTS):
+            entries = slot_list[:, e0 * C // LIST_ROWS : (e0 + count) * C // LIST_ROWS]
+            codes = keep.tile([P, count * C], U32, name="codes%d" % i, align_bytes=64)
+            scale = keep.tile([P, count * C], U8, name="scale%d" % i, align_bytes=64)
+            nc.vector.tensor_copy(codes[:], x_codes[:].indirect(entries))
+            nc.vector.tensor_copy(scale[:], x_scale[:].indirect(entries))
+            for j in range(count):
+                slot_codes[e0 + j] = codes[:, j * C : (j + 1) * C]
+                slot_scale[e0 + j] = scale[:, j * C : (j + 1) * C]
+            expert_rows(range(e0, e0 + count), 0)
+            e0 = e0 + count
+
+        def gated(nb, t0, width):
+            prods = []
+            for r in range(TOP):
+                prod = work.tile([P, BANK], F32, name="prod%d" % r)
+                entries = pos_list[r][:, t0 // LIST_ROWS : (t0 + width) // LIST_ROWS]
+                nc.vector.tensor_tensor(prod[:, :width], y[nb][:].indirect(entries), gate_rows[r][:, t0 : t0 + width], MULT)
+                prods.append(prod)
+            return prods
+
+        def combine_on_tensor(nb, t0, width):
+            prods = gated(nb, t0, width)
+            turned = sum_psum.tile([P, BANK], F32)
+            for c0 in range(0, width, P):
+                for r in range(TOP):
+                    nc.tensor.matmul(
+                        turned[:, c0 : c0 + P], prods[r][:, c0 : c0 + P], ident[:],
+                        start=(r == 0), stop=(r == TOP - 1), is_transpose=True,
+                    )
+            turned_sb = work.tile([P, BANK], F32)
+            nc.scalar.copy(turned_sb[:, :width], turned[:, :width])
+            back = back_psum.tile([P, BANK], F32)
+            for c0 in range(0, width, P):
+                nc.tensor.transpose(back[:, c0 : c0 + P], turned_sb[:, c0 : c0 + P], ident[:])
+            result = work.tile([P, BANK], F32)
+            nc.scalar.copy(result[:, :width], back[:, :width])
+            nc.sync.dma_start(out=out[nb * P : (nb + 1) * P, t0 : t0 + width], in_=result[:, :width])
+
+        def combine_on_vector(nb, t0, width):
+            prods = gated(nb, t0, width)
+            pair = work.tile([P, BANK], F32)
+            nc.vector.tensor_tensor(pair[:, :width], prods[0][:, :width], prods[1][:, :width], ADD)
+            total = work.tile([P, BANK], F32)
+            nc.vector.tensor_tensor(total[:, :width], pair[:, :width], prods[2][:, :width], ADD)
+            nc.sync.dma_start(out=out[nb * P : (nb + 1) * P, t0 : t0 + width], in_=total[:, :width])
+
+        for nb in range(BLOCKS):
+            if nb + 1 < BLOCKS:
+                for e0 in range(0, E, 4):
+                    expert_rows(range(e0, e0 + 4), nb + 1)
+                combine_on_tensor(nb, 0, 512)
+                combine_on_tensor(nb, 512, 512)
+            else:
+                combine_on_tensor(nb, 0, 512)
+                combine_on_tensor(nb, 512, 256)
+                combine_on_vector(nb, 768, 256)

@@ -28,7 +28,6 @@ BLOCKS = N // P
 BANK = 512
 
 X_LOADS = (512, 256, 256)
-GATHER_EXPERTS = (4, 4, 4, 3, 1)
 W_LOAD_EXPERTS = 8
 
 
@@ -36,18 +35,17 @@ def tile_moe_ecr_lin_gelu_kernel(tc, xT, w_words, w_scales, b, gate, offs, pos1,
     nc = tc.nc
     with ExitStack() as ctx:
         keep = ctx.enter_context(tc.tile_pool(name="keep", bufs=1))
-        work = ctx.enter_context(tc.tile_pool(name="work", bufs=3))
-        mm_psum = ctx.enter_context(tc.psum_pool(name="mm_psum", bufs=4))
-        sum_psum = ctx.enter_context(tc.psum_pool(name="sum_psum", bufs=2))
+        work = ctx.enter_context(tc.tile_pool(name="work", bufs=4))
+        sum_psum = ctx.enter_context(tc.psum_pool(name="sum_psum", bufs=6))
         back_psum = ctx.enter_context(tc.psum_pool(name="back_psum", bufs=2))
 
+        zeros = keep.tile([P, PAD], F32)
+        nc.vector.memset(zeros[:], 0.0)
         w_scale = keep.tile([P, E, N], U8, align_bytes=64)
         nc.vector.memset(w_scale[:].bitcast(I32), 0)
         x_codes = keep.tile([P, T], U32, align_bytes=64)
         x_scale = keep.tile([P, T], U8, align_bytes=64)
         nc.vector.memset(x_scale[:].bitcast(I32), 0)
-        zeros = keep.tile([P, PAD], F32)
-        nc.vector.memset(zeros[:], 0.0)
 
         x_rows = xT.rearrange("(p j) t -> p j t", j=PACK)
         x_raw = []
@@ -60,6 +58,13 @@ def tile_moe_ecr_lin_gelu_kernel(tc, xT, w_words, w_scales, b, gate, offs, pos1,
 
         slot_list = keep.tile([P, SLOTS // LIST_ROWS], U16)
         nc.sync.dma_start(slot_list[:], offs)
+        pos_list = []
+        for r, pos in enumerate((pos1, pos2, pos3)):
+            pl = keep.tile([P, T // LIST_ROWS], U16, name="pos_list%d" % r)
+            nc.sync.dma_start(pl[:], pos)
+            pos_list.append(pl)
+        bias = keep.tile([P, BLOCKS, E], F32)
+        nc.sync.dma_start(out=bias[:], in_=b.rearrange("(c p) e -> p c e", p=P))
 
         for r in range(4):
             nc.sync.dma_start(
@@ -74,14 +79,8 @@ def tile_moe_ecr_lin_gelu_kernel(tc, xT, w_words, w_scales, b, gate, offs, pos1,
                 in_=w_words[i * W_LOAD_EXPERTS : (i + 1) * W_LOAD_EXPERTS, 0, :, :].rearrange("e p c -> p e c").bitcast(I32),
             )
             w_code.append(wt)
-        bias = keep.tile([P, BLOCKS, E], F32)
-        nc.sync.dma_start(out=bias[:], in_=b.rearrange("(c p) e -> p c e", p=P))
-        pos_list = []
         gate_rows = []
-        for r, pos in enumerate((pos1, pos2, pos3)):
-            pl = keep.tile([P, T // LIST_ROWS], U16, name="pos_list%d" % r)
-            nc.sync.dma_start(pl[:], pos)
-            pos_list.append(pl)
+        for r in range(TOP):
             g = keep.tile([P, T], F32, name="gate_rows%d" % r)
             nc.sync.dma_start(out=g[:], in_=gate[r, 0:P, :])
             gate_rows.append(g)
@@ -108,20 +107,20 @@ def tile_moe_ecr_lin_gelu_kernel(tc, xT, w_words, w_scales, b, gate, offs, pos1,
                 in_=grouped[:].rearrange("p c j -> p (c j)"),
             )
 
-        ga = interleave(nc.vector.tensor_copy, "ga", x_raw[0], 0, 512)
-        gb = interleave(nc.scalar.copy, "gb", x_raw[1], 0, 256)
-        quantize(ga, 0, 512)
-        gc = interleave(nc.vector.tensor_copy, "gc", x_raw[2], 0, 128)
-        gd = interleave(nc.scalar.copy, "gd", x_raw[2], 128, 128)
-        quantize(gb, 512, 256)
-        quantize(gc, 768, 128)
-        quantize(gd, 896, 128)
+        t0 = 0
+        for i, width in enumerate(X_LOADS):
+            half = width // 2
+            on_vector = interleave(nc.vector.tensor_copy, "grouped_v%d" % i, x_raw[i], 0, half)
+            on_scalar = interleave(nc.scalar.copy, "grouped_s%d" % i, x_raw[i], half, half)
+            quantize(on_vector, t0, half)
+            quantize(on_scalar, t0 + half, half)
+            t0 = t0 + width
 
         slot_codes = {}
         slot_scale = {}
 
         def expert_rows(experts, nb):
-            acc = mm_psum.tile([P, BANK], F32)
+            acc = sum_psum.tile([P, BANK], F32, name="acc")
             for i, e in enumerate(experts):
                 wt = w_code[e // W_LOAD_EXPERTS]
                 nc.tensor.matmul_mx(
@@ -138,39 +137,35 @@ def tile_moe_ecr_lin_gelu_kernel(tc, xT, w_words, w_scales, b, gate, offs, pos1,
                     y[nb][:, e * C : (e + 1) * C], acc[:, i * C : (i + 1) * C], GELU, bias=bias[:, nb, e : e + 1]
                 )
 
-        e0 = 0
-        for i, count in enumerate(GATHER_EXPERTS):
+        def gather_slots(table, store, dtype, name, e0, count):
             entries = slot_list[:, e0 * C // LIST_ROWS : (e0 + count) * C // LIST_ROWS]
-            codes = keep.tile([P, count * C], U32, name="codes%d" % i, align_bytes=64)
-            scale = keep.tile([P, count * C], U8, name="scale%d" % i, align_bytes=64)
-            nc.vector.tensor_copy(codes[:], x_codes[:].indirect(entries))
-            nc.vector.tensor_copy(scale[:], x_scale[:].indirect(entries))
+            got = keep.tile([P, count * C], dtype, name="%s%d" % (name, e0), align_bytes=64)
+            nc.vector.tensor_copy(got[:], table[:].indirect(entries))
             for j in range(count):
-                slot_codes[e0 + j] = codes[:, j * C : (j + 1) * C]
-                slot_scale[e0 + j] = scale[:, j * C : (j + 1) * C]
-            expert_rows(range(e0, e0 + count), 0)
-            e0 = e0 + count
+                store[e0 + j] = got[:, j * C : (j + 1) * C]
 
-        def gated(nb, t0, width):
-            prods = []
-            for r in range(TOP):
-                prod = work.tile([P, BANK], F32, name="prod%d" % r)
-                entries = pos_list[r][:, t0 // LIST_ROWS : (t0 + width) // LIST_ROWS]
-                nc.vector.tensor_tensor(prod[:, :width], y[nb][:].indirect(entries), gate_rows[r][:, t0 : t0 + width], MULT)
-                prods.append(prod)
-            return prods
+        for e0, pieces in ((0, (6,)), (6, (6,)), (12, (2, 1, 1))):
+            gather_slots(x_codes, slot_codes, U32, "codes", e0, sum(pieces))
+            e1 = e0
+            for count in pieces:
+                gather_slots(x_scale, slot_scale, U8, "scale", e1, count)
+                for e2 in range(e1, e1 + count, 3):
+                    expert_rows(range(e2, min(e2 + 3, e1 + count)), 0)
+                e1 = e1 + count
+            if e0 == 0:
+                expert_rows(range(0, 3), 1)
+                expert_rows(range(3, 6), 1)
 
-        def combine_on_tensor(nb, t0, width):
-            prods = gated(nb, t0, width)
-            turned = sum_psum.tile([P, BANK], F32)
-            for c0 in range(0, width, P):
-                for r in range(TOP):
-                    nc.tensor.matmul(
-                        turned[:, c0 : c0 + P], prods[r][:, c0 : c0 + P], ident[:],
-                        start=(r == 0), stop=(r == TOP - 1), is_transpose=True,
-                    )
-            turned_sb = work.tile([P, BANK], F32)
-            nc.scalar.copy(turned_sb[:, :width], turned[:, :width])
+        def gated(nb, r, t0, width):
+            prod = work.tile([P, T], F32, name="prod%d" % r)
+            entries = pos_list[r][:, t0 // LIST_ROWS : (t0 + width) // LIST_ROWS]
+            nc.vector.tensor_tensor(prod[:, :width], y[nb][:].indirect(entries), gate_rows[r][:, t0 : t0 + width], MULT)
+            return prod
+
+        def add_turned(turned, part, r):
+            nc.tensor.matmul(turned, part, ident[:], start=(r == 0), stop=(r == TOP - 1), is_transpose=True)
+
+        def turn_back(nb, t0, width, turned_sb):
             back = back_psum.tile([P, BANK], F32)
             for c0 in range(0, width, P):
                 nc.tensor.transpose(back[:, c0 : c0 + P], turned_sb[:, c0 : c0 + P], ident[:])
@@ -178,21 +173,50 @@ def tile_moe_ecr_lin_gelu_kernel(tc, xT, w_words, w_scales, b, gate, offs, pos1,
             nc.scalar.copy(result[:, :width], back[:, :width])
             nc.sync.dma_start(out=out[nb * P : (nb + 1) * P, t0 : t0 + width], in_=result[:, :width])
 
-        def combine_on_vector(nb, t0, width):
-            prods = gated(nb, t0, width)
-            pair = work.tile([P, BANK], F32)
-            nc.vector.tensor_tensor(pair[:, :width], prods[0][:, :width], prods[1][:, :width], ADD)
-            total = work.tile([P, BANK], F32)
-            nc.vector.tensor_tensor(total[:, :width], pair[:, :width], prods[2][:, :width], ADD)
-            nc.sync.dma_start(out=out[nb * P : (nb + 1) * P, t0 : t0 + width], in_=total[:, :width])
+        def sum_bank(nb, t0, parts):
+            turned = sum_psum.tile([P, BANK], F32, name="acc")
+            for c0 in range(0, BANK, P):
+                for r in range(TOP):
+                    add_turned(turned[:, c0 : c0 + P], parts[r][:, c0 : c0 + P], r)
+            turned_sb = work.tile([P, BANK], F32)
+            nc.scalar.copy(turned_sb[:], turned[:])
+            turn_back(nb, t0, BANK, turned_sb)
 
-        for nb in range(BLOCKS):
-            if nb + 1 < BLOCKS:
-                for e0 in range(0, E, 4):
-                    expert_rows(range(e0, e0 + 4), nb + 1)
-                combine_on_tensor(nb, 0, 512)
-                combine_on_tensor(nb, 512, 512)
-            else:
-                combine_on_tensor(nb, 0, 512)
-                combine_on_tensor(nb, 512, 256)
-                combine_on_vector(nb, 768, 256)
+        expert_rows(range(6, 10), 1)
+        expert_rows(range(10, 13), 1)
+        expert_rows(range(13, 16), 1)
+        for e0 in range(0, E, 4):
+            expert_rows(range(e0, e0 + 4), 2)
+
+        prods = [gated(0, r, 0, T) for r in range(TOP)]
+        for t0 in (0, BANK):
+            sum_bank(0, t0, [p[:, t0 : t0 + BANK] for p in prods])
+
+        prods = [gated(1, r, 0, T) for r in range(TOP - 1)]
+        for t0 in (0, BANK):
+            last = gated(1, TOP - 1, t0, BANK)
+            sum_bank(1, t0, [p[:, t0 : t0 + BANK] for p in prods] + [last[:, :BANK]])
+
+        wide = 640
+        turned = [sum_psum.tile([P, P], F32, name="acc") for c in range(wide // P)]
+        turned_sb = work.tile([P, wide], F32, name="turned_wide")
+        for r in range(TOP):
+            prod = gated(2, r, 0, wide)
+            for c in range(wide // P):
+                add_turned(turned[c][:], prod[:, c * P : (c + 1) * P], r)
+                if r == TOP - 1:
+                    nc.scalar.copy(turned_sb[:, c * P : (c + 1) * P], turned[c][:])
+        turn_back(2, 0, BANK, turned_sb[:, :BANK])
+        turn_back(2, BANK, wide - BANK, turned_sb[:, BANK:])
+
+        width = T - wide
+        half = width // 2
+        prods = [gated(2, r, wide, width) for r in range(TOP)]
+        pair = work.tile([P, width], F32)
+        for c0 in (0, half):
+            nc.vector.tensor_tensor(pair[:, c0 : c0 + half], prods[0][:, c0 : c0 + half], prods[1][:, c0 : c0 + half], ADD)
+        for c0 in (0, half):
+            total = work.tile([P, half], F32)
+            nc.vector.tensor_tensor(total[:], pair[:, c0 : c0 + half], prods[2][:, c0 : c0 + half], ADD)
+            queue = nc.sync if c0 == 0 else nc.scalar
+            queue.dma_start(out=out[2 * P :, wide + c0 : wide + c0 + half], in_=total[:])

@@ -218,5 +218,4 @@ def tile_moe_ecr_lin_gelu_kernel(tc, xT, w_words, w_scales, b, gate, offs, pos1,
         for c0 in (0, half):
             total = work.tile([P, half], F32)
             nc.vector.tensor_tensor(total[:], pair[:, c0 : c0 + half], prods[2][:, c0 : c0 + half], ADD)
-            queue = nc.sync if c0 == 0 else nc.scalar
-            queue.dma_start(out=out[2 * P :, wide + c0 : wide + c0 + half], in_=total[:])
+            nc.sync.dma_start(out=out[2 * P :, wide + c0 : wide + c0 + half], in_=total[:])

from contextlib import ExitStack

import concourse.mybir as mybir
from concourse.masks import make_identity

K, T, E, C, N = 512, 1024, 16, 128, 384
TOP = 3
PAD = 64
SLOTS = E * C
FLOPS = 2 * K * N * SLOTS

F32 = mybir.dt.float32
BF16 = mybir.dt.bfloat16
I32 = mybir.dt.int32
U32 = mybir.dt.uint32
U16 = mybir.dt.uint16
U8 = mybir.dt.uint8
FP8X4 = mybir.dt.float8_e4m3fn_x4
FP4X4 = mybir.dt.float4_e2m1fn_x4
GELU = mybir.ActivationFunctionType.Gelu_apprx_tanh
MULT = mybir.AluOpType.mult
ADD = mybir.AluOpType.add

P = 128
PACK = 4
LIST_ROWS = 16
BLOCKS = N // P
BANK = 512

X_LOADS = (512, 256, 256)
W_LOAD_EXPERTS = 8


def tile_moe_ecr_lin_gelu_kernel(tc, xT, w_words, w_scales, b, gate, offs, pos1, pos2, pos3, out):
    nc = tc.nc
    with ExitStack() as ctx:
        keep = ctx.enter_context(tc.tile_pool(name="keep", bufs=1))
        work = ctx.enter_context(tc.tile_pool(name="work", bufs=4))
        sum_psum = ctx.enter_context(tc.psum_pool(name="sum_psum", bufs=6))
        back_psum = ctx.enter_context(tc.psum_pool(name="back_psum", bufs=2))

        zeros = keep.tile([P, PAD], F32)
        nc.vector.memset(zeros[:], 0.0)
        w_scale = keep.tile([P, E, N], U8, align_bytes=64)
        nc.vector.memset(w_scale[:].bitcast(I32), 0)
        x_codes = keep.tile([P, T], U32, align_bytes=64)
        x_scale = keep.tile([P, T], U8, align_bytes=64)
        nc.vector.memset(x_scale[:].bitcast(I32), 0)

        x_rows = xT.rearrange("(p j) t -> p j t", j=PACK)
        x_raw = []
        t0 = 0
        for i, width in enumerate(X_LOADS):
            raw = keep.tile([P, PACK, width], F32, name="x_raw%d" % i)
            nc.sync.dma_start(out=raw[:], in_=x_rows[:, :, t0 : t0 + width])
            x_raw.append(raw)
            t0 = t0 + width

        slot_list = keep.tile([P, SLOTS // LIST_ROWS], U16)
        nc.sync.dma_start(slot_list[:], offs)
        pos_list = []
        for r, pos in enumerate((pos1, pos2, pos3)):
            pl = keep.tile([P, T // LIST_ROWS], U16, name="pos_list%d" % r)
            nc.sync.dma_start(pl[:], pos)
            pos_list.append(pl)
        bias = keep.tile([P, BLOCKS, E], F32)
        nc.sync.dma_start(out=bias[:], in_=b.rearrange("(c p) e -> p c e", p=P))

        for r in range(4):
            nc.sync.dma_start(
                out=w_scale[r:P:32, :, :].bitcast(I32),
                in_=w_scales[:, 0, r:16:4, :].rearrange("e q n -> q e n").bitcast(I32),
            )
        w_code = []
        for i in range(E // W_LOAD_EXPERTS):
            wt = keep.tile([P, W_LOAD_EXPERTS, 2 * N], U8, name="w_code%d" % i, align_bytes=64)
            nc.sync.dma_start(
                out=wt[:].bitcast(I32),
                in_=w_words[i * W_LOAD_EXPERTS : (i + 1) * W_LOAD_EXPERTS, 0, :, :].rearrange("e p c -> p e c").bitcast(I32),
            )
            w_code.append(wt)
        gate_rows = []
        for r in range(TOP):
            g = keep.tile([P, T], F32, name="gate_rows%d" % r)
            nc.sync.dma_start(out=g[:], in_=gate[r, 0:P, :])
            gate_rows.append(g)

        ident = keep.tile([P, P], F32)
        make_identity(nc, ident[:])

        y = [keep.tile([P, SLOTS + PAD], F32, name="y%d" % nb) for nb in range(BLOCKS)]
        for nb in range(BLOCKS):
            nc.scalar.activation(y[nb][:, SLOTS:], zeros[:], GELU)

        def interleave(copy, name, raw, c0, width):
            grouped = keep.tile([P, width, PACK], BF16, name=name, align_bytes=64)
            copy(
                grouped[:].rearrange("p (c i) j -> p c j i", i=4),
                raw[:, :, c0 : c0 + width].rearrange("p j (c i) -> p c j i", i=4),
            )
            return grouped

        def quantize(grouped, t0, width):
            nc.vector.quantize_mx(
                out=x_codes[:, t0 : t0 + width].bitcast(FP8X4),
                scales=x_scale[:, t0 : t0 + width],
                in_=grouped[:].rearrange("p c j -> p (c j)"),
            )

        t0 = 0
        for i, width in enumerate(X_LOADS):
            half = width // 2
            on_vector = interleave(nc.vector.tensor_copy, "grouped_v%d" % i, x_raw[i], 0, half)
            on_scalar = interleave(nc.scalar.copy, "grouped_s%d" % i, x_raw[i], half, half)
            quantize(on_vector, t0, half)
            quantize(on_scalar, t0 + half, half)
            t0 = t0 + width

        slot_codes = {}
        slot_scale = {}

        def expert_rows(experts, nb):
            acc = sum_psum.tile([P, BANK], F32, name="acc")
            for i, e in enumerate(experts):
                wt = w_code[e // W_LOAD_EXPERTS]
                nc.tensor.matmul_mx(
                    out=acc[:, i * C : (i + 1) * C],
                    lhsT=wt[:, e % W_LOAD_EXPERTS, 2 * nb * P : 2 * (nb + 1) * P].bitcast(FP4X4),
                    lhsT_scale=w_scale[:, e, nb * P : (nb + 1) * P],
                    rhs=slot_codes[e].bitcast(FP8X4),
                    rhs_scale=slot_scale[e],
                    start=True,
                    stop=True,
                )
            for i, e in enumerate(experts):
                nc.scalar.activation(
                    y[nb][:, e * C : (e + 1) * C], acc[:, i * C : (i + 1) * C], GELU, bias=bias[:, nb, e : e + 1]
                )

        def gather_slots(table, store, dtype, name, e0, count):
            entries = slot_list[:, e0 * C // LIST_ROWS : (e0 + count) * C // LIST_ROWS]
            got = keep.tile([P, count * C], dtype, name="%s%d" % (name, e0), align_bytes=64)
            nc.vector.tensor_copy(got[:], table[:].indirect(entries))
            for j in range(count):
                store[e0 + j] = got[:, j * C : (j + 1) * C]

        for e0, pieces in ((0, (6,)), (6, (6,)), (12, (2, 1, 1))):
            gather_slots(x_codes, slot_codes, U32, "codes", e0, sum(pieces))
            e1 = e0
            for count in pieces:
                gather_slots(x_scale, slot_scale, U8, "scale", e1, count)
                for e2 in range(e1, e1 + count, 3):
                    expert_rows(range(e2, min(e2 + 3, e1 + count)), 0)
                e1 = e1 + count
            if e0 == 0:
                expert_rows(range(0, 3), 1)
                expert_rows(range(3, 6), 1)

        def gated(nb, r, t0, width):
            prod = work.tile([P, T], F32, name="prod%d" % r)
            entries = pos_list[r][:, t0 // LIST_ROWS : (t0 + width) // LIST_ROWS]
            nc.vector.tensor_tensor(prod[:, :width], y[nb][:].indirect(entries), gate_rows[r][:, t0 : t0 + width], MULT)
            return prod

        def add_turned(turned, part, r):
            nc.tensor.matmul(turned, part, ident[:], start=(r == 0), stop=(r == TOP - 1), is_transpose=True)

        def turn_back(nb, t0, width, turned_sb):
            back = back_psum.tile([P, BANK], F32)
            for c0 in range(0, width, P):
                nc.tensor.transpose(back[:, c0 : c0 + P], turned_sb[:, c0 : c0 + P], ident[:])
            result = work.tile([P, BANK], F32)
            nc.scalar.copy(result[:, :width], back[:, :width])
            nc.sync.dma_start(out=out[nb * P : (nb + 1) * P, t0 : t0 + width], in_=result[:, :width])

        def sum_bank(nb, t0, parts):
            turned = sum_psum.tile([P, BANK], F32, name="acc")
            for c0 in range(0, BANK, P):
                for r in range(TOP):
                    add_turned(turned[:, c0 : c0 + P], parts[r][:, c0 : c0 + P], r)
            turned_sb = work.tile([P, BANK], F32)
            nc.scalar.copy(turned_sb[:], turned[:])
            turn_back(nb, t0, BANK, turned_sb)

        expert_rows(range(6, 10), 1)
        expert_rows(range(10, 13), 1)
        expert_rows(range(13, 16), 1)
        for e0 in range(0, E, 4):
            expert_rows(range(e0, e0 + 4), 2)

        prods = [gated(0, r, 0, T) for r in range(TOP)]
        for t0 in (0, BANK):
            sum_bank(0, t0, [p[:, t0 : t0 + BANK] for p in prods])

        prods = [gated(1, r, 0, T) for r in range(TOP - 1)]
        for t0 in (0, BANK):
            last = gated(1, TOP - 1, t0, BANK)
            sum_bank(1, t0, [p[:, t0 : t0 + BANK] for p in prods] + [last[:, :BANK]])

        wide = 640
        turned = [sum_psum.tile([P, P], F32, name="acc") for c in range(wide // P)]
        turned_sb = work.tile([P, wide], F32, name="turned_wide")
        for r in range(TOP):
            prod = gated(2, r, 0, wide)
            for c in range(wide // P):
                add_turned(turned[c][:], prod[:, c * P : (c + 1) * P], r)
                if r == TOP - 1:
                    nc.scalar.copy(turned_sb[:, c * P : (c + 1) * P], turned[c][:])
        turn_back(2, 0, BANK, turned_sb[:, :BANK])
        turn_back(2, BANK, wide - BANK, turned_sb[:, BANK:])

        width = T - wide
        half = width // 2
        prods = [gated(2, r, wide, width) for r in range(TOP)]
        pair = work.tile([P, width], F32)
        for c0 in (0, half):
            nc.vector.tensor_tensor(pair[:, c0 : c0 + half], prods[0][:, c0 : c0 + half], prods[1][:, c0 : c0 + half], ADD)
        for c0 in (0, half):
            total = work.tile([P, half], F32)
            nc.vector.tensor_tensor(total[:], pair[:, c0 : c0 + half], prods[2][:, c0 : c0 + half], ADD)
            nc.sync.dma_start(out=out[2 * P :, wide + c0 : wide + c0 + half], in_=total[:])
